import numpy as np
CORES = [0,1,2,3,4,5,6,7,8,9,10,11,12,13,14,15,16,17,18,19,20,21,22,23,24,25,26,27,28,29,30,31,32,33,34,35,36,37,38,39,40,41,42,43,44,45,46,47,48,49,50,51,52,53,54,55,56,57,58,59,60,61,62,63,64,65,66,67,68,69,70,71,72,73,74,75,76,77,78,79,80,81,82,83,84,85,86,87,88,89,90,91,92,93,94,95,96,97,98,99,100,101,102,103,104,105,106,107,108,109,110,111,112,113,114,115,116,117,118,119,120,121,122,123,124,125,126,127,128,129,130,131,132,133,134,135,136,137,138,139,140,141,142,143,144,145,146,147,148,149,150,151,152,153,154,155,156,157,158,159,160,161,162,163,164,165,166,167,168,169,170,171,172,173,174,175,176,177,178,179,180,181,182,183,184,185,186,187,188,189,190,191,192,193,194,195,196,197,198,199,200,201,202,203,204,205,206,207,208,209,210,211,212,213,214,215,216,217,218,219,220,221,222,223,224,225,226,227,228,229,230,231,232,233,234,235,236,237,238,239,240,241,242,243,244,245,246,247,248,249,250,251,252,253,254,255]
N = 256
PAIRS = [[16 * p + i for i in range(16)] for p in range(16)]
ACROSS = [[8 * c + (k if c % 2 == 0 else k ^ 2) for c in range(32)] for k in range(8)]
def setup_inputs(rng):
    return {"x1": rng.standard_normal((N, 128, 32), dtype=np.float32), "x2": rng.standard_normal((N, 128, 256), dtype=np.float32)}
def reference(x1, x2):
    y1 = np.empty((N, 128, 16 * 32), x1.dtype)
    for g in PAIRS:
        cat = np.concatenate([x1[r] for r in g], axis=1)
        for r in g:
            y1[r] = cat
    y2 = np.empty_like(x2)
    for g in ACROSS:
        s = x2[g].sum(axis=0, dtype=np.float64).astype(x2.dtype)
        for r in g:
            y2[r] = s
    return {"y1": y1, "y2": y2}

import concourse.bass as bass

A_N = (29, 28)
B_N = (3, 4)

SCRATCH = {
    "g1": ("sbuf", [128, 512], "float32"),
    "xa0": ("dram", [8, 128, 29], "float32"),
    "xa1": ("dram", [8, 128, 28], "float32"),
    "na0": ("dram", [8, 128, 29], "float32"),
    "na1": ("dram", [8, 128, 28], "float32"),
    "ra0": ("dram", [8, 128, 29], "float32"),
    "ra1": ("dram", [8, 128, 28], "float32"),
    "ya0": ("dram", [8, 128, 29], "float32"),
    "ya1": ("dram", [8, 128, 28], "float32"),
    "xb0": ("dram", [8, 128, 3], "float32"),
    "xb1": ("dram", [8, 128, 4], "float32"),
    "rb0": ("dram", [16, 128, 3], "float32"),
    "rb1": ("dram", [16, 128, 4], "float32"),
    "mb0": ("dram", [128, 3], "float32"),
    "mb1": ("dram", [128, 4], "float32"),
    "hb0": ("dram", [128, 3], "float32"),
    "hb1": ("dram", [128, 4], "float32"),
    "tb0": ("dram", [128, 3], "float32"),
    "tb1": ("dram", [128, 4], "float32"),
    "yb0": ("dram", [8, 128, 3], "float32"),
    "yb1": ("dram", [8, 128, 4], "float32"),
}
SEMAPHORES = ["ld", "st", "sent", "g1a", "g2a", "g3a", "a1", "a2", "a3", "a4", "a5", "b1", "b2", "b3", "b4t", "by"]


def rank_program(g, core, T, topo):
    S = T.sem
    h, ch, k = core // 128, (core % 128) // 8, core % 8
    q, j = ch % 2, ch // 2
    die0 = k & 4
    port = (k & 2) != 0
    c = k & 1

    def here(kk):
        return core - k + kk

    def mate(kk):
        return h * 128 + (ch ^ 1) * 8 + kk

    def plane(jj, kk):
        return h * 128 + (2 * jj + q) * 8 + kk

    def twin(kk):
        return (1 - h) * 128 + ch * 8 + kk

    owed = [0]

    def tr(srcs, dsts, sem, mask):
        ids = []
        for d, ap in dsts:
            rid, pid = topo.addr(d, core)
            ids.append(bass.DstId(rid=rid, pnc=pid))
        owed[0] += bin(mask).count("1")
        return bass.RemoteDMATransfer(dst_ids=ids, dma_engine_mask=mask, remote_sem=sem, srcs=srcs,
                                      dsts=[ap for d, ap in dsts], alu_op=1 if len(srcs) > 1 else 0)

    def call(*transfers):
        g.remote_dma_fused(list(transfers), local_sem=S.sent)

    def blocks(first, n=1):
        return T.g1[:, 32 * first:32 * (first + n)]

    xa, na, ra, ya = (T.xa0, T.xa1)[c], (T.na0, T.na1)[c], (T.ra0, T.ra1)[c], (T.ya0, T.ya1)[c]
    xb, yb, tb = (T.xb0, T.xb1)[c], (T.yb0, T.yb1)[c], (T.tb0, T.tb1)[c]
    rows_a = 4 * A_N[c]
    others = [here(i) for i in range(8) if i != k]
    mine = blocks(8 * q + k)

    g.dma_start(mine, T.x1[:]).then_inc(S.ld, 16)
    g.dma_start(xa[:], T.x2[0:rows_a, :]).then_inc(S.ld, 16)
    g.dma_start(xb[:], T.x2[rows_a:128, :]).then_inc(S.ld, 16)
    g.wait_ge(S.ld, 48)

    call(tr([mine], [(d, mine) for d in others], S.g1a, 0xFFFF))
    owner = die0 + 3 - c
    half = 8 if port else 0
    rb_c = (T.rb0, T.rb1)[c]
    call(*[tr([xb[jj]], [(plane(jj, owner), rb_c[half + j])], S.b1, 1 << jj) for jj in range(8)])

    if port:
        oc = 1 - c
        rb, mb, hb = (T.rb0, T.rb1)[oc], (T.mb0, T.mb1)[oc], (T.hb0, T.hb1)[oc]
        yb_o, tb_o = (T.yb0, T.yb1)[oc], (T.tb0, T.tb1)[oc]
        call(*[tr([xa[n]], [(mate(k - 2), na[n])], S.a1, 1 << n) for n in range(8)])
        g.wait_ge(S.g1a, 7 * 16)
        two = blocks(8 * q + die0 + 2 * c, 2)
        call(tr([two], [(mate(k - 2), two)], S.g2a, 0xFF))
        g.wait_ge(S.b1, 16)
        call(tr([rb[8 + n] for n in range(8)], [(mate(k), mb[:])], S.b2, 0xFF))
        g.wait_ge(S.b2, 8)
        kept = [rb[n] for n in range(8)] + [mb[:]]
        call(tr(kept, [(twin(k), hb[:])], S.b3, 0xFF))
        g.wait_ge(S.b3, 8)
        kept = kept + [hb[:]]
        call(tr(kept, [(plane(jj, die0 + oc), yb_o[j]) for jj in range(8)], S.by, 0x0F),
             tr(kept, [(mate(die0 + oc), tb_o[:])], S.b4t, 0xF0))
        g.wait_ge(S.a4, 8 * 8)
        call(*[tr([na[n]], [(here(k - 2), ya[n]), (mate(k), ya[n])], S.a5, 1 << n) for n in range(8)])
        g.wait_ge(S.g3a, 4 * 16)
        g.wait_ge(S.by, 8 * 8)
    else:
        g.wait_ge(S.a1, 8)
        call(*[tr([xa[jj], na[jj]], [(plane(jj, k), ra[j])], S.a2, 1 << n)
               for n, jj in enumerate([x for x in range(8) if x != j])])
        g.wait_ge(S.g2a, 8)
        two = blocks(8 * (1 - q) + die0 + 2 * c, 2)
        call(tr([two], [(d, two) for d in others], S.g3a, 0xFFFF))
        g.wait_ge(S.a2, 7)
        part = [xa[j], na[j]] + [ra[x] for x in range(8) if x != j]
        call(tr(part, [(twin(k), ra[j])], S.a3, 0xFF))
        g.wait_ge(S.a3, 8)
        call(tr(part + [ra[j]], [(plane(jj, k + 2), na[j]) for jj in range(8)], S.a4, 0xFF))
        g.wait_ge(S.b4t, 4)
        call(tr([tb[:]], [(plane(jj, k + 2), yb[j]) for jj in range(8)], S.by, 0xFF))
        g.wait_ge(S.g1a, 7 * 16)
        g.wait_ge(S.g3a, 3 * 16)
        g.wait_ge(S.by, 8 * 4)

    g.dma_start(T.y1[:], T.g1[:]).then_inc(S.st, 16)
    g.dma_start(T.y2[rows_a:128, :], yb[:]).then_inc(S.st, 16)
    g.wait_ge(S.a5, 8)
    g.dma_start(T.y2[0:rows_a, :], ya[:]).then_inc(S.st, 16)
    g.wait_ge(S.st, 48)
    g.wait_ge(S.sent, owed[0])
